import numpy as np
import ml_dtypes


def mxq(x, axis, fmt="e4m3"):
    dtype, down = {"e4m3": (ml_dtypes.float8_e4m3fn, 7), "e5m2": (ml_dtypes.float8_e5m2, 14)}[fmt]
    v = np.moveaxis(np.asarray(x, np.float32).astype(ml_dtypes.bfloat16).astype(np.float64), axis, -1)
    blocks = v.reshape(v.shape[:-1] + (-1, 32))
    amax = np.abs(blocks).max(-1, keepdims=True)
    byte = np.maximum(np.where(amax > 0, np.frexp(amax)[1] - 1 + 127, 0) - down, 1)
    scale = np.exp2(byte - 127.0)
    codes = (blocks / scale).astype(np.float32).astype(dtype).astype(np.float64)
    return np.moveaxis((codes * scale).reshape(v.shape), -1, axis)


WIDE = False


def mx_kscale(k):
    if not WIDE:
        return np.ones(k)
    levels = np.array([10, -10, 5, -5, 0])
    if k % 512:
        return np.exp2(np.random.permutation(np.resize(levels, k // 32))).repeat(32)
    a = np.empty((k // 512, 16))
    for p in range(k // 512):
        a[p, :8] = np.random.permutation(np.resize(levels, 8))
        for g in range(8):
            far = levels[np.abs(levels - a[p, g]) >= 10]
            a[p, g + 8] = far[np.random.randint(len(far))]
    return np.exp2(a.ravel()).repeat(32)


def f64(x):
    return np.asarray(x).astype(np.float64)


def striped(idx):
    return np.tile(np.asarray(idx).reshape(-1, 16).T, (8, 1)).astype(np.uint16)


def unstriped(offs):
    return offs[:16].T.reshape(-1).astype(np.int64)


E2M1 = np.array([0.0, 0.5, 1.0, 1.5, 2.0, 3.0, 4.0, 6.0, -0.0, -0.5, -1.0, -1.5, -2.0, -3.0, -4.0, -6.0])


def pack_weight(w, fmt):
    k, n = w.shape
    w = f64(np.asarray(w, np.float32).astype(ml_dtypes.bfloat16)).reshape(k // 32, 32, n)
    amax = np.abs(w).max(1)
    if fmt == "e4m3":
        byte = np.frexp(amax)[1] - 1 + 127 - 7
    else:
        mant, ex = np.frexp(amax / 6.0)
        byte = np.where(mant > 0.5, ex, ex - 1) + 127
    byte = np.clip(np.where(amax > 0, byte, 1), 1, 254)
    scaled = (w * np.exp2(127.0 - byte)[:, None, :]).reshape(k, n).astype(np.float32)
    by_word = np.ascontiguousarray(scaled.reshape(k // 512, 128, 4, n).transpose(0, 1, 3, 2))
    if fmt == "e4m3":
        words = by_word.astype(ml_dtypes.float8_e4m3fn).view(np.uint8)
    else:
        c = by_word.astype(ml_dtypes.float4_e2m1fn).view(np.uint8) & 0xF
        words = (c[..., 0::2] | (c[..., 1::2] << 4)).reshape(k // 512, 128, 2 * n)
    return np.ascontiguousarray(words), np.ascontiguousarray(byte.astype(np.uint8).reshape(k // 512, 16, n))


def unpack_weight(words, scales, fmt):
    g, _, n = scales.shape
    words = np.ascontiguousarray(words).reshape(g, 128, n, -1)
    if fmt == "e4m3":
        vals = words.view(ml_dtypes.float8_e4m3fn).astype(np.float64)
    else:
        nib = np.empty((g, 128, n, 4), np.uint8)
        nib[..., 0::2] = words & 0xF
        nib[..., 1::2] = words >> 4
        vals = E2M1[nib]
    vals = vals * np.repeat(np.exp2(scales.astype(np.float64) - 127.0), 8, axis=1)[..., None]
    return vals.transpose(0, 1, 3, 2).reshape(g * 512, n)


def bf(x):
    return np.asarray(x, np.float32).astype(ml_dtypes.bfloat16)


def planes(Y):
    r, m = Y.shape
    b = f64(bf(Y)).reshape(r // 32, 32, m)
    amax = np.abs(b).max(1)
    byte = np.clip(np.where(amax > 0, np.frexp(amax)[1] - 1 + 127 - 7, 1), 1, 254)
    codes = (b * np.exp2(127.0 - byte)[:, None, :]).reshape(r, m).astype(np.float32).astype(ml_dtypes.float8_e4m3fn).view(np.uint8)
    words = codes.reshape(r // 512, 128, 4, m).transpose(0, 1, 3, 2)
    return np.ascontiguousarray(words), np.ascontiguousarray(byte.astype(np.uint8).reshape(r // 512, 16, m))


D, T, I, J, U, E, M = 512, 2048, 512, 512, 1024, 512, 1024


def setup_inputs():
    n = np.random.standard_normal
    idx = np.random.permutation(T)[:I]
    idx2 = np.random.permutation(U)[:J]
    idx3 = np.random.permutation(M)[:J]
    fd = mx_kscale(D)
    fi = mx_kscale(I)
    ti = np.ones(T)
    ti[idx] = fi
    keysp = pack_weight(n((D, T)) / fd[:, None], "e2m1")
    return {
        "keys_words": keysp[0],
        "keys_scales": keysp[1],
        "notes": (n((D, U)) * 1.0 / np.sqrt(D) * fd[:, None]).astype(np.float32),
        "rowf": (np.random.uniform(0.02, 0.08, (I, 1)) * fi[:, None]).astype(np.float32),
        "vals": (n((E, T)) / ti).astype(np.float32),
        "old": (1.0 * n((E, M))).astype(np.float32),
        "offs": striped(idx),
        "offs2": striped(idx2),
        "offs3": striped(idx3),
    }


def reference(keys_words, keys_scales, notes, rowf, vals, old, offs, offs2, offs3):
    idx = unstriped(offs)
    idx2 = unstriped(offs2)
    idx3 = unstriped(offs3)
    keysu = unpack_weight(keys_words, keys_scales, "e2m1")
    keysidxg = keysu[:, idx]
    notesidx2q = mxq(f64(notes)[:, idx2], 0, "e4m3")
    g9 = keysidxg.T @ notesidx2q
    g0 = np.maximum(g9, 0.0)
    gr1 = g0 * f64(rowf)
    vt1 = f64(vals)[:, idx].T
    vt1q = mxq(vt1, 0, "e4m3")
    gr1q = mxq(gr1, 0, "e4m3")
    o = vt1q.T @ gr1q
    of = np.zeros((E, M))
    of[:, idx3] = o
    y = f64(old) + of
    words, scales = planes(y)
    return y, words, scales

@@ -1,0 +1,249 @@
+from contextlib import ExitStack
+
+import concourse.mybir as mybir
+from concourse.masks import make_identity
+
+D, T, I, J, U, E, M = 512, 2048, 512, 512, 1024, 512, 1024
+FLOPS = 2 * D * I * J + 2 * I * E * J
+
+F32 = mybir.dt.float32
+BF16 = mybir.dt.bfloat16
+I32 = mybir.dt.int32
+U32 = mybir.dt.uint32
+U16 = mybir.dt.uint16
+U8 = mybir.dt.uint8
+FP8X4 = mybir.dt.float8_e4m3fn_x4
+FP4X4 = mybir.dt.float4_e2m1fn_x4
+COPY = mybir.ActivationFunctionType.Copy
+ALU = mybir.AluOpType
+
+P = 128
+PACK = 4
+LIST_COLS = 32
+CHUNK = 128
+OUT_CHUNK = 256
+
+
+def gather_on_scalar(nc, out, window, offsets):
+    nc.scalar.activation(out, window.indirect(offsets), COPY)
+
+
+def gather_on_vector(nc, out, window, offsets):
+    nc.vector.tensor_copy(out, window.indirect(offsets))
+
+
+def weave(copy, woven, planes):
+    copy(woven.rearrange("p (c i) t -> p c t i", i=4), planes.rearrange("p t (c i) -> p c t i", i=4))
+
+
+def tile_attend_tab_plain_put_pl_kernel(tc, keys_words, keys_scales, notes, rowf, vals, old, offs, offs2, offs3, out_0, out_1, out_2):
+    nc = tc.nc
+    notes_rows = notes.rearrange("(p t) u -> p t u", t=PACK)
+    vals_rows = vals.rearrange("(p t) c -> p t c", t=PACK)
+    old_rows = old.rearrange("(p t) m -> p t m", t=PACK)
+    out_rows = out_0.rearrange("(p t) m -> p t m", t=PACK)
+    out_words = out_1[0].rearrange("p m r -> p (m r)").bitcast(I32)
+
+    with ExitStack() as ctx:
+        sb = ctx.enter_context(tc.tile_pool(name="sb", bufs=1))
+        ps = ctx.enter_context(tc.psum_pool(name="ps", bufs=1))
+
+        tokens = sb.tile([P, LIST_COLS], U16)
+        picked_notes = sb.tile([P, LIST_COLS], U16)
+        places = sb.tile([P, LIST_COLS], U16)
+        key_words = sb.tile([P, T], U16)
+        key_bytes = sb.tile([P, T], U8)
+        factors = sb.tile([P, PACK], F32)
+        note_pool = [sb.tile([P, U], F32, name=f"note_pool{t}") for t in range(PACK)]
+        val_pool = [sb.tile([P, T], F32, name=f"val_pool{t}", tag=f"val_pool{t}", align_bytes=64) for t in range(PACK)]
+        before = [sb.tile([P, M], F32, name=f"before{t}") for t in range(PACK)]
+        put = [sb.tile([P, M], F32, name=f"put{t}") for t in range(PACK)]
+        identity = sb.tile([P, P], F32)
+
+        for t in range(PACK):
+            nc.vector.memset(put[t][:], 0.0)
+        make_identity(nc, identity[:])
+
+        nc.sync.dma_start(tokens[:], offs)
+        nc.sync.dma_start(key_words[:].bitcast(I32), keys_words[0].bitcast(I32))
+        for q in range(4):
+            rows = keys_scales[0, 4 * q : 4 * q + 4, :].bitcast(I32)
+            nc.scalar.dma_start(key_bytes[32 * q : 32 * q + 32, :].bitcast(I32), rows.unsqueeze(0).to_broadcast([8, 4, T // 4]))
+        nc.sync.dma_start(picked_notes[:], offs2)
+        for t in range(PACK):
+            nc.sync.dma_start(note_pool[t][:], notes_rows[:, t, :])
+        nc.sync.dma_start(factors[:], rowf.rearrange("(p t) o -> p (t o)", t=PACK))
+        nc.sync.dma_start(val_pool[0][:], vals_rows[:, 0, :])
+        nc.sync.dma_start(places[:], offs3)
+        for t in range(1, PACK):
+            nc.sync.dma_start(val_pool[t][:], vals_rows[:, t, :])
+        for t in range(PACK):
+            nc.sync.dma_start(before[t][:], old_rows[:, t, :])
+
+        words_listed = sb.tile([P, I], U16, align_bytes=64)
+        words_dealt = sb.tile([P, PACK, P], U16, align_bytes=64)
+        bytes_dealt = sb.tile([P, PACK, P], U8, align_bytes=64)
+        gather_on_vector(nc, words_listed[:], key_words[:], tokens[:])
+        nc.vector.tensor_copy(words_dealt[:], words_listed[:].rearrange("p (s r) -> p r s", r=PACK))
+        gather_on_vector(nc, bytes_dealt[:].rearrange("p r s -> p s r"), key_bytes[:], tokens[:])
+
+        half = J // 2
+        note_planes = sb.tile([P, PACK, J], BF16, align_bytes=64)
+        for t in range(2):
+            gather_on_scalar(nc, note_planes[:, t, :], note_pool[t][:], picked_notes[:])
+        gather_on_vector(nc, note_planes[:, 2, :], note_pool[2][:], picked_notes[:])
+        last = PACK - 1
+        gather_on_vector(nc, note_planes[:, last, :half], note_pool[last][:], picked_notes[:, : LIST_COLS // 2])
+        gather_on_scalar(nc, note_planes[:, last, half:], note_pool[last][:], picked_notes[:, LIST_COLS // 2 :])
+
+        note_codes = sb.tile([P, J], U32, align_bytes=64)
+        note_scales = sb.tile([P, J], U8, align_bytes=64)
+        chunks = [slice(c * CHUNK, (c + 1) * CHUNK) for c in range(J // CHUNK)]
+        notes_woven = [sb.tile([P, CHUNK, PACK], BF16, name=f"notes_woven{c}", align_bytes=64) for c in range(len(chunks))]
+        table = [sb.tile([P, CHUNK, PACK], BF16, name=f"table{c}", align_bytes=64) for c in range(len(chunks))]
+        table_codes = sb.tile([P, J], U32, align_bytes=64)
+        table_scales = sb.tile([P, J], U8, align_bytes=64)
+        raw = [None] * len(chunks)
+
+        def quantise_notes(c):
+            nc.vector.quantize_mx(out=note_codes[:, chunks[c]].bitcast(FP8X4), scales=note_scales[:, chunks[c]], in_=notes_woven[c][:].rearrange("p j t -> p (j t)"))
+            raw[c] = ps.tile([P, PACK, CHUNK], F32, name="raw", tag="raw", bufs=3)
+            for r in range(PACK):
+                nc.tensor.matmul_mx(
+                    out=raw[c][:, r, :],
+                    lhsT=words_dealt[:, r, :].bitcast(FP4X4),
+                    lhsT_scale=bytes_dealt[:, r, :],
+                    rhs=note_codes[:, chunks[c]].bitcast(FP8X4),
+                    rhs_scale=note_scales[:, chunks[c]],
+                    start=True,
+                    stop=True,
+                )
+
+        def weigh(c):
+            nc.vector.scalar_tensor_tensor(
+                out=table[c][:],
+                in0=raw[c][:].rearrange("p r j -> p j r"),
+                scalar=0.0,
+                in1=factors[:].unsqueeze(1).to_broadcast([P, CHUNK, PACK]),
+                op0=ALU.max,
+                op1=ALU.mult,
+            )
+
+        def quantise_table(c):
+            nc.vector.quantize_mx(out=table_codes[:, chunks[c]].bitcast(FP8X4), scales=table_scales[:, chunks[c]], in_=table[c][:].rearrange("p j r -> p (j r)"))
+
+        for c in range(2):
+            weave(nc.vector.tensor_copy, notes_woven[c][:], note_planes[:, :, chunks[c]])
+            weave(nc.scalar.copy, notes_woven[c + 2][:], note_planes[:, :, chunks[c + 2]])
+        quantise_notes(0)
+        quantise_notes(1)
+        quantise_notes(2)
+        weigh(0)
+        quantise_notes(3)
+        for c in range(1, len(chunks)):
+            weigh(c)
+            quantise_table(c - 1)
+        quantise_table(len(chunks) - 1)
+
+        result = sb.tile([P, PACK, M], F32)
+        val_codes = [None] * PACK
+        val_scales = [None] * PACK
+        acc = [None] * PACK
+        listed = [None] * PACK
+        product = {}
+
+        def gather_values(t):
+            listed[t] = sb.tile([P, I], BF16, name=f"listed{t}", tag=f"listed{t}", align_bytes=64)
+            gather_on_scalar(nc, listed[t][:], val_pool[t][:], tokens[:])
+
+        def turn_values(t, copy):
+            pairs = listed[t][:].bitcast(F32)
+            turned = ps.tile([P, 2, P], F32, name="turned", tag="shared" if t == 1 else "turned", bufs=1 if t == 1 else 2)
+            for u in range(2):
+                nc.tensor.transpose(turned[:, u, :], pairs[:, u : I // 2 : 2], identity[:])
+            woven = sb.tile([P, P * PACK], BF16, name=f"vals_woven{t}", tag=f"woven{t}", align_bytes=64)
+            copy(woven[:].bitcast(F32).rearrange("p (e u) -> p e u", u=2), turned[:].rearrange("p u e -> p e u"))
+            val_codes[t] = sb.tile([P, P], U32, name=f"val_codes{t}", align_bytes=64)
+            val_scales[t] = sb.tile([P, P], U8, name=f"val_scales{t}", align_bytes=64)
+            nc.vector.quantize_mx(out=val_codes[t][:].bitcast(FP8X4), scales=val_scales[t][:], in_=woven[:])
+
+        def multiply(t):
+            acc[t] = ps.tile([P, J], F32, name="acc", tag="shared" if t == 0 else "acc", bufs=1 if t == 0 else 2)
+            nc.tensor.matmul_mx(
+                out=acc[t][:],
+                lhsT=val_codes[t][:].bitcast(FP8X4),
+                lhsT_scale=val_scales[t][:],
+                rhs=table_codes[:].bitcast(FP8X4),
+                rhs_scale=table_scales[:],
+                start=True,
+                stop=True,
+            )
+
+        def copy_out(copy, t, h, tag):
+            product[t, h] = sb.tile([P, half], F32, name=f"product{t}_{h}", tag=tag, align_bytes=64)
+            copy(product[t, h][:], acc[t][:, h * half : (h + 1) * half])
+
+        def copy_out_whole(t, tag):
+            both = sb.tile([P, J], F32, name=f"product{t}", tag=tag, align_bytes=64)
+            nc.scalar.copy(both[:], acc[t][:])
+            for h in range(2):
+                product[t, h] = both[:, h * half : (h + 1) * half]
+
+        def scatter_on_vector(t, h):
+            nc.vector.tensor_copy(put[t][:].indirect(places[:, h * 16 : (h + 1) * 16]), product[t, h][:])
+
+        def scatter_on_scalar(t, h):
+            nc.scalar.activation(put[t][:].indirect(places[:, h * 16 : (h + 1) * 16]), product[t, h], COPY)
+
+        def add_and_store(t, cols):
+            nc.vector.tensor_tensor(result[:, t, cols], before[t][:, cols], put[t][:, cols], ALU.add)
+            nc.sync.dma_start(out_rows[:, t, cols], result[:, t, cols])
+
+        on_vector = nc.vector.tensor_copy
+        on_scalar = nc.scalar.copy
+        whole = slice(0, M)
+        gather_values(0)
+        turn_values(0, on_scalar)
+        gather_values(1)
+        turn_values(1, on_scalar)
+        multiply(0)
+        copy_out(on_vector, 0, 0, "woven1")
+        scatter_on_vector(0, 0)
+        gather_values(2)
+        multiply(1)
+        turn_values(2, on_scalar)
+        copy_out(on_scalar, 1, 1, "val_pool2")
+        copy_out(on_vector, 0, 1, "woven2")
+        scatter_on_vector(0, 1)
+        gather_values(3)
+        multiply(2)
+        copy_out_whole(2, "val_pool3")
+        turn_values(3, on_vector)
+        copy_out(on_vector, 1, 0, "woven3")
+        scatter_on_scalar(2, 0)
+        scatter_on_vector(1, 0)
+        multiply(3)
+        scatter_on_scalar(2, 1)
+        scatter_on_vector(1, 1)
+        add_and_store(0, whole)
+        copy_out_whole(3, "product3")
+        scatter_on_scalar(3, 0)
+        scatter_on_scalar(3, 1)
+        add_and_store(1, whole)
+        add_and_store(2, whole)
+        add_and_store(3, slice(0, M // 2))
+        add_and_store(3, slice(M // 2, M))
+
+        result_codes = sb.tile([P, M], U32, align_bytes=64)
+        result_scales = sb.tile([P, M], U8, align_bytes=64)
+        for c in range(M // OUT_CHUNK):
+            cols = slice(c * OUT_CHUNK, (c + 1) * OUT_CHUNK)
+            rounded = sb.tile([P, OUT_CHUNK, PACK], BF16, name=f"rounded{c}", align_bytes=64)
+            weave(nc.scalar.copy if c % 2 == 0 else nc.vector.tensor_copy, rounded[:], result[:, :, cols])
+            nc.vector.quantize_mx(out=result_codes[:, cols].bitcast(FP8X4), scales=result_scales[:, cols], in_=rounded[:].rearrange("p m t -> p (m t)"))
+            if c % 2 == 1:
+                both = slice((c - 1) * OUT_CHUNK, (c + 1) * OUT_CHUNK)
+                nc.sync.dma_start(out_words[:, both], result_codes[:, both].bitcast(I32))
+        for q in range(4):
+            queue = nc.sync if q % 2 == 0 else nc.scalar
+            queue.dma_start(out_2[0, 4 * q : 4 * q + 4, :].bitcast(I32), result_scales[32 * q : 32 * q + 4, :].bitcast(I32))

@@ -56,7 +56,7 @@ def tile_attend_tab_plain_put_pl_kernel(tc, keys_words, keys_scales, notes, rowf
         factors = sb.tile([P, PACK], F32)
         note_pool = [sb.tile([P, U], F32, name=f"note_pool{t}") for t in range(PACK)]
         val_pool = [sb.tile([P, T], F32, name=f"val_pool{t}", tag=f"val_pool{t}", align_bytes=64) for t in range(PACK)]
-        before = [sb.tile([P, M], F32, name=f"before{t}") for t in range(PACK)]
+        before = {t: sb.tile([P, M], F32, name=f"before{t}") for t in (0, 2, 3)}
         put = [sb.tile([P, M], F32, name=f"put{t}") for t in range(PACK)]
         identity = sb.tile([P, P], F32)
 
@@ -65,47 +65,49 @@ def tile_attend_tab_plain_put_pl_kernel(tc, keys_words, keys_scales, notes, rowf
         make_identity(nc, identity[:])
 
         nc.sync.dma_start(tokens[:], offs)
-        nc.sync.dma_start(key_words[:].bitcast(I32), keys_words[0].bitcast(I32))
         for q in range(4):
             rows = keys_scales[0, 4 * q : 4 * q + 4, :].bitcast(I32)
             nc.scalar.dma_start(key_bytes[32 * q : 32 * q + 32, :].bitcast(I32), rows.unsqueeze(0).to_broadcast([8, 4, T // 4]))
         nc.sync.dma_start(picked_notes[:], offs2)
         for t in range(PACK):
             nc.sync.dma_start(note_pool[t][:], notes_rows[:, t, :])
+        nc.sync.dma_start(key_words[:].bitcast(I32), keys_words[0].bitcast(I32))
         nc.sync.dma_start(factors[:], rowf.rearrange("(p t) o -> p (t o)", t=PACK))
         nc.sync.dma_start(val_pool[0][:], vals_rows[:, 0, :])
         nc.sync.dma_start(places[:], offs3)
         for t in range(1, PACK):
             nc.sync.dma_start(val_pool[t][:], vals_rows[:, t, :])
-        for t in range(PACK):
+        for t in (0, 2, 3):
             nc.sync.dma_start(before[t][:], old_rows[:, t, :])
 
-        words_listed = sb.tile([P, I], U16, align_bytes=64)
+        words_listed = sb.tile([P, I], U16, tag="words_listed", align_bytes=64)
         words_dealt = sb.tile([P, PACK, P], U16, align_bytes=64)
         bytes_dealt = sb.tile([P, PACK, P], U8, align_bytes=64)
-        gather_on_vector(nc, words_listed[:], key_words[:], tokens[:])
-        nc.vector.tensor_copy(words_dealt[:], words_listed[:].rearrange("p (s r) -> p r s", r=PACK))
         gather_on_vector(nc, bytes_dealt[:].rearrange("p r s -> p s r"), key_bytes[:], tokens[:])
 
         half = J // 2
-        note_planes = sb.tile([P, PACK, J], BF16, align_bytes=64)
+        note_planes = sb.tile([P, PACK, J], BF16, tag="note_planes", align_bytes=64)
         for t in range(2):
             gather_on_scalar(nc, note_planes[:, t, :], note_pool[t][:], picked_notes[:])
         gather_on_vector(nc, note_planes[:, 2, :], note_pool[2][:], picked_notes[:])
         last = PACK - 1
         gather_on_vector(nc, note_planes[:, last, :half], note_pool[last][:], picked_notes[:, : LIST_COLS // 2])
         gather_on_scalar(nc, note_planes[:, last, half:], note_pool[last][:], picked_notes[:, LIST_COLS // 2 :])
+        gather_on_vector(nc, words_listed[:], key_words[:], tokens[:])
+        nc.vector.tensor_copy(words_dealt[:], words_listed[:].rearrange("p (s r) -> p r s", r=PACK))
 
-        note_codes = sb.tile([P, J], U32, align_bytes=64)
+        note_codes = sb.tile([P, J], U32, tag="words_listed", align_bytes=64)
         note_scales = sb.tile([P, J], U8, align_bytes=64)
         chunks = [slice(c * CHUNK, (c + 1) * CHUNK) for c in range(J // CHUNK)]
+        halves = [slice(0, half), slice(half, J)]
+        every = slice(0, J)
         notes_woven = [sb.tile([P, CHUNK, PACK], BF16, name=f"notes_woven{c}", align_bytes=64) for c in range(len(chunks))]
-        table = [sb.tile([P, CHUNK, PACK], BF16, name=f"table{c}", align_bytes=64) for c in range(len(chunks))]
-        table_codes = sb.tile([P, J], U32, align_bytes=64)
+        table = [sb.tile([P, half, PACK], BF16, name=f"table{h}", tag=("table0", "relay")[h], align_bytes=64) for h in range(2)]
+        table_codes = {}
         table_scales = sb.tile([P, J], U8, align_bytes=64)
-        raw = [None] * len(chunks)
+        raw = {}
 
-        def quantise_notes(c):
+        def score(c):
             nc.vector.quantize_mx(out=note_codes[:, chunks[c]].bitcast(FP8X4), scales=note_scales[:, chunks[c]], in_=notes_woven[c][:].rearrange("p j t -> p (j t)"))
             raw[c] = ps.tile([P, PACK, CHUNK], F32, name="raw", tag="raw", bufs=3)
             for r in range(PACK):
@@ -121,7 +123,7 @@ def tile_attend_tab_plain_put_pl_kernel(tc, keys_words, keys_scales, notes, rowf
 
         def weigh(c):
             nc.vector.scalar_tensor_tensor(
-                out=table[c][:],
+                out=table[c // 2][:, chunks[c % 2], :],
                 in0=raw[c][:].rearrange("p r j -> p j r"),
                 scalar=0.0,
                 in1=factors[:].unsqueeze(1).to_broadcast([P, CHUNK, PACK]),
@@ -129,110 +131,132 @@ def tile_attend_tab_plain_put_pl_kernel(tc, keys_words, keys_scales, notes, rowf
                 op1=ALU.mult,
             )
 
-        def quantise_table(c):
-            nc.vector.quantize_mx(out=table_codes[:, chunks[c]].bitcast(FP8X4), scales=table_scales[:, chunks[c]], in_=table[c][:].rearrange("p j r -> p (j r)"))
-
-        for c in range(2):
-            weave(nc.vector.tensor_copy, notes_woven[c][:], note_planes[:, :, chunks[c]])
-            weave(nc.scalar.copy, notes_woven[c + 2][:], note_planes[:, :, chunks[c + 2]])
-        quantise_notes(0)
-        quantise_notes(1)
-        quantise_notes(2)
-        weigh(0)
-        quantise_notes(3)
-        for c in range(1, len(chunks)):
-            weigh(c)
-            quantise_table(c - 1)
-        quantise_table(len(chunks) - 1)
+        def quantise_table(h, tag):
+            table_codes[h] = sb.tile([P, half], U32, name=f"table_codes{h}", tag=tag, align_bytes=64)
+            nc.vector.quantize_mx(out=table_codes[h][:].bitcast(FP8X4), scales=table_scales[:, halves[h]], in_=table[h][:].rearrange("p j r -> p (j r)"))
 
         result = sb.tile([P, PACK, M], F32)
-        val_codes = [None] * PACK
-        val_scales = [None] * PACK
-        acc = [None] * PACK
-        listed = [None] * PACK
+        listed = {}
+        woven = {}
+        val_codes = {}
+        val_scales = {}
+        acc = {}
         product = {}
 
-        def gather_values(t):
-            listed[t] = sb.tile([P, I], BF16, name=f"listed{t}", tag=f"listed{t}", align_bytes=64)
-            gather_on_scalar(nc, listed[t][:], val_pool[t][:], tokens[:])
+        def gather_values(gather, t, tag):
+            listed[t] = sb.tile([P, I], BF16, name=f"listed{t}", tag=tag, align_bytes=64)
+            gather(nc, listed[t][:], val_pool[t][:], tokens[:])
 
-        def turn_values(t, copy):
+        def turn_values(t, bank_tag, into):
             pairs = listed[t][:].bitcast(F32)
-            turned = ps.tile([P, 2, P], F32, name="turned", tag="shared" if t == 1 else "turned", bufs=1 if t == 1 else 2)
+            turned = ps.tile([P, 2, P], F32, name="turned", tag=bank_tag, bufs=3 if bank_tag == "raw" else 1)
             for u in range(2):
                 nc.tensor.transpose(turned[:, u, :], pairs[:, u : I // 2 : 2], identity[:])
-            woven = sb.tile([P, P * PACK], BF16, name=f"vals_woven{t}", tag=f"woven{t}", align_bytes=64)
-            copy(woven[:].bitcast(F32).rearrange("p (e u) -> p e u", u=2), turned[:].rearrange("p u e -> p e u"))
+            woven[t] = into.bitcast(BF16)
+            nc.vector.tensor_copy(into.rearrange("p (e u) -> p e u", u=2), turned[:].rearrange("p u e -> p e u"))
+
+        def quantise_values(t):
             val_codes[t] = sb.tile([P, P], U32, name=f"val_codes{t}", align_bytes=64)
             val_scales[t] = sb.tile([P, P], U8, name=f"val_scales{t}", align_bytes=64)
-            nc.vector.quantize_mx(out=val_codes[t][:].bitcast(FP8X4), scales=val_scales[t][:], in_=woven[:])
+            nc.vector.quantize_mx(out=val_codes[t][:].bitcast(FP8X4), scales=val_scales[t][:], in_=woven[t])
 
-        def multiply(t):
-            acc[t] = ps.tile([P, J], F32, name="acc", tag="shared" if t == 0 else "acc", bufs=1 if t == 0 else 2)
-            nc.tensor.matmul_mx(
-                out=acc[t][:],
-                lhsT=val_codes[t][:].bitcast(FP8X4),
-                lhsT_scale=val_scales[t][:],
-                rhs=table_codes[:].bitcast(FP8X4),
-                rhs_scale=table_scales[:],
-                start=True,
-                stop=True,
-            )
+        def multiply(t, which, bank_tag):
+            bank = ps.tile([P, J], F32, name="acc", tag=bank_tag, bufs=3 if bank_tag == "raw" else 1)
+            for h in which:
+                nc.tensor.matmul_mx(
+                    out=bank[:, halves[h]],
+                    lhsT=val_codes[t][:].bitcast(FP8X4),
+                    lhsT_scale=val_scales[t][:],
+                    rhs=table_codes[h][:].bitcast(FP8X4),
+                    rhs_scale=table_scales[:, halves[h]],
+                    start=True,
+                    stop=True,
+                )
+                acc[t, h] = bank
 
-        def copy_out(copy, t, h, tag):
-            product[t, h] = sb.tile([P, half], F32, name=f"product{t}_{h}", tag=tag, align_bytes=64)
-            copy(product[t, h][:], acc[t][:, h * half : (h + 1) * half])
+        def copy_half(copy, t, h, into):
+            copy(into, acc[t, h][:, halves[h]])
+            product[t, h] = into
 
-        def copy_out_whole(t, tag):
-            both = sb.tile([P, J], F32, name=f"product{t}", tag=tag, align_bytes=64)
-            nc.scalar.copy(both[:], acc[t][:])
+        def copy_whole(copy, t, into):
+            copy(into, acc[t, 0][:])
             for h in range(2):
-                product[t, h] = both[:, h * half : (h + 1) * half]
+                product[t, h] = into[:, halves[h]]
+
+        def reuse(tag, cols):
+            return sb.tile([P, cols], F32, name="reused_" + tag, tag=tag, align_bytes=64)[:]
 
         def scatter_on_vector(t, h):
-            nc.vector.tensor_copy(put[t][:].indirect(places[:, h * 16 : (h + 1) * 16]), product[t, h][:])
+            nc.vector.tensor_copy(put[t][:].indirect(places[:, h * 16 : (h + 1) * 16]), product[t, h])
+
+        def scatter_whole_on_vector(t, source):
+            nc.vector.tensor_copy(put[t][:].indirect(places[:]), source)
 
         def scatter_on_scalar(t, h):
             nc.scalar.activation(put[t][:].indirect(places[:, h * 16 : (h + 1) * 16]), product[t, h], COPY)
 
-        def add_and_store(t, cols):
-            nc.vector.tensor_tensor(result[:, t, cols], before[t][:, cols], put[t][:, cols], ALU.add)
-            nc.sync.dma_start(out_rows[:, t, cols], result[:, t, cols])
+        def add_and_store(engine, t):
+            engine.tensor_tensor(result[:, t, :], before[t][:], put[t][:], ALU.add)
+            nc.sync.dma_start(out_rows[:, t, :], result[:, t, :])
 
         on_vector = nc.vector.tensor_copy
         on_scalar = nc.scalar.copy
-        whole = slice(0, M)
-        gather_values(0)
-        turn_values(0, on_scalar)
-        gather_values(1)
-        turn_values(1, on_scalar)
-        multiply(0)
-        copy_out(on_vector, 0, 0, "woven1")
-        scatter_on_vector(0, 0)
-        gather_values(2)
-        multiply(1)
-        turn_values(2, on_scalar)
-        copy_out(on_scalar, 1, 1, "val_pool2")
-        copy_out(on_vector, 0, 1, "woven2")
-        scatter_on_vector(0, 1)
-        gather_values(3)
-        multiply(2)
-        copy_out_whole(2, "val_pool3")
-        turn_values(3, on_vector)
-        copy_out(on_vector, 1, 0, "woven3")
-        scatter_on_scalar(2, 0)
-        scatter_on_vector(1, 0)
-        multiply(3)
-        scatter_on_scalar(2, 1)
-        scatter_on_vector(1, 1)
-        add_and_store(0, whole)
-        copy_out_whole(3, "product3")
+        for c in range(len(chunks)):
+            weave(on_scalar, notes_woven[c][:], note_planes[:, :, chunks[c]])
+        gather_values(gather_on_scalar, 0, "note_planes")
+        score(0)
+        score(1)
+        score(2)
+        weigh(0)
+        score(3)
+        weigh(1)
+        turn_values(0, "raw", reuse("woven0", half))
+        weigh(2)
+        quantise_table(0, "table_codes0")
+        quantise_values(0)
+        weigh(3)
+        gather_values(gather_on_scalar, 1, "listed1")
+        multiply(0, [0], "bank_a")
+        quantise_table(1, "woven0")
+        multiply(0, [1], "bank_b")
+        first = reuse("val_pool1", J)
+        copy_half(on_scalar, 0, 0, first[:, :half])
+        scatter_on_scalar(0, 0)
+        copy_half(on_scalar, 0, 1, first[:, half:])
+        scatter_on_scalar(0, 1)
+
+        gather_values(gather_on_vector, 2, "relay")
+        turn_values(1, "raw", reuse("val_pool2", half))
+        quantise_values(1)
+        multiply(1, [0, 1], "bank_c")
+        gather_values(gather_on_vector, 3, "val_pool2")
+        relay = reuse("val_pool3", half + J)
+        turn_values(2, "bank_d", relay[:, :half])
+        copy_whole(on_vector, 1, relay[:, half:])
+        quantise_values(2)
+        turn_values(3, "bank_e", reuse("woven3", half))
+        before[1] = sb.tile([P, M], F32, name="before1", tag="val_pool2", align_bytes=64)
+        nc.sync.dma_start(before[1][:], old_rows[:, 1, :])
+        multiply(2, [0, 1], "raw")
+        quantise_values(3)
+        multiply(3, [0, 1], "raw")
+        scatter_on_scalar(1, 0)
+        scatter_on_scalar(1, 1)
+        third = reuse("woven3", J)
+        copy_whole(on_vector, 2, third)
+        add_and_store(nc.vector, 0)
+        scatter_whole_on_vector(2, third)
+        copy_whole(on_scalar, 3, reuse("product3", J))
         scatter_on_scalar(3, 0)
         scatter_on_scalar(3, 1)
-        add_and_store(1, whole)
-        add_and_store(2, whole)
-        add_and_store(3, slice(0, M // 2))
-        add_and_store(3, slice(M // 2, M))
+        add_and_store(nc.vector, 1)
+        add_and_store(nc.vector, 2)
+        for c in range(M // OUT_CHUNK):
+            cols = slice(c * OUT_CHUNK, (c + 1) * OUT_CHUNK)
+            nc.vector.tensor_tensor(result[:, 3, cols], before[3][:, cols], put[3][:, cols], ALU.add)
+            if c % 2 == 1:
+                both = slice((c - 1) * OUT_CHUNK, (c + 1) * OUT_CHUNK)
+                nc.sync.dma_start(out_rows[:, 3, both], result[:, 3, both])
 
         result_codes = sb.tile([P, M], U32, align_bytes=64)
         result_scales = sb.tile([P, M], U8, align_bytes=64)
@@ -241,9 +265,7 @@ def tile_attend_tab_plain_put_pl_kernel(tc, keys_words, keys_scales, notes, rowf
             rounded = sb.tile([P, OUT_CHUNK, PACK], BF16, name=f"rounded{c}", align_bytes=64)
             weave(nc.scalar.copy if c % 2 == 0 else nc.vector.tensor_copy, rounded[:], result[:, :, cols])
             nc.vector.quantize_mx(out=result_codes[:, cols].bitcast(FP8X4), scales=result_scales[:, cols], in_=rounded[:].rearrange("p m t -> p (m t)"))
-            if c % 2 == 1:
-                both = slice((c - 1) * OUT_CHUNK, (c + 1) * OUT_CHUNK)
-                nc.sync.dma_start(out_words[:, both], result_codes[:, both].bitcast(I32))
+            nc.sync.dma_start(out_words[:, cols], result_codes[:, cols].bitcast(I32))
         for q in range(4):
             queue = nc.sync if q % 2 == 0 else nc.scalar
             queue.dma_start(out_2[0, 4 * q : 4 * q + 4, :].bitcast(I32), result_scales[32 * q : 32 * q + 4, :].bitcast(I32))

@@ -62,20 +62,19 @@ def tile_attend_tab_plain_put_pl_kernel(tc, keys_words, keys_scales, notes, rowf
 
         for t in range(PACK):
             nc.vector.memset(put[t][:], 0.0)
+        nc.gpsimd.memset(key_bytes[:].bitcast(I32), 0)
         make_identity(nc, identity[:])
 
         nc.sync.dma_start(tokens[:], offs)
-        for q in range(4):
-            rows = keys_scales[0, 4 * q : 4 * q + 4, :].bitcast(I32)
-            nc.scalar.dma_start(key_bytes[32 * q : 32 * q + 32, :].bitcast(I32), rows.unsqueeze(0).to_broadcast([8, 4, T // 4]))
         nc.sync.dma_start(picked_notes[:], offs2)
+        nc.sync.dma_start(places[:], offs3)
+        nc.sync.dma_start(factors[:], rowf.rearrange("(p t) o -> p (t o)", t=PACK))
+        for q in range(4):
+            nc.scalar.dma_start(key_bytes[32 * q : 32 * q + 4, :].bitcast(I32), keys_scales[0, 4 * q : 4 * q + 4, :].bitcast(I32))
         for t in range(PACK):
             nc.sync.dma_start(note_pool[t][:], notes_rows[:, t, :])
         nc.sync.dma_start(key_words[:].bitcast(I32), keys_words[0].bitcast(I32))
-        nc.sync.dma_start(factors[:], rowf.rearrange("(p t) o -> p (t o)", t=PACK))
-        nc.sync.dma_start(val_pool[0][:], vals_rows[:, 0, :])
-        nc.sync.dma_start(places[:], offs3)
-        for t in range(1, PACK):
+        for t in range(PACK):
             nc.sync.dma_start(val_pool[t][:], vals_rows[:, t, :])
         for t in (0, 2, 3):
             nc.sync.dma_start(before[t][:], old_rows[:, t, :])

from contextlib import ExitStack

import concourse.mybir as mybir
from concourse.masks import make_identity

D, T, I, J, U, E, M = 512, 2048, 512, 512, 1024, 512, 1024
FLOPS = 2 * D * I * J + 2 * I * E * J

F32 = mybir.dt.float32
BF16 = mybir.dt.bfloat16
I32 = mybir.dt.int32
U32 = mybir.dt.uint32
U16 = mybir.dt.uint16
U8 = mybir.dt.uint8
FP8X4 = mybir.dt.float8_e4m3fn_x4
FP4X4 = mybir.dt.float4_e2m1fn_x4
COPY = mybir.ActivationFunctionType.Copy
ALU = mybir.AluOpType

P = 128
PACK = 4
LIST_COLS = 32
CHUNK = 128
OUT_CHUNK = 256


def gather_on_scalar(nc, out, window, offsets):
    nc.scalar.activation(out, window.indirect(offsets), COPY)


def gather_on_vector(nc, out, window, offsets):
    nc.vector.tensor_copy(out, window.indirect(offsets))


def weave(copy, woven, planes):
    copy(woven.rearrange("p (c i) t -> p c t i", i=4), planes.rearrange("p t (c i) -> p c t i", i=4))


def tile_attend_tab_plain_put_pl_kernel(tc, keys_words, keys_scales, notes, rowf, vals, old, offs, offs2, offs3, out_0, out_1, out_2):
    nc = tc.nc
    notes_rows = notes.rearrange("(p t) u -> p t u", t=PACK)
    vals_rows = vals.rearrange("(p t) c -> p t c", t=PACK)
    old_rows = old.rearrange("(p t) m -> p t m", t=PACK)
    out_rows = out_0.rearrange("(p t) m -> p t m", t=PACK)
    out_words = out_1[0].rearrange("p m r -> p (m r)").bitcast(I32)

    with ExitStack() as ctx:
        sb = ctx.enter_context(tc.tile_pool(name="sb", bufs=1))
        ps = ctx.enter_context(tc.psum_pool(name="ps", bufs=1))

        tokens = sb.tile([P, LIST_COLS], U16)
        picked_notes = sb.tile([P, LIST_COLS], U16)
        places = sb.tile([P, LIST_COLS], U16)
        key_words = sb.tile([P, T], U16)
        key_bytes = sb.tile([P, T], U8)
        factors = sb.tile([P, PACK], F32)
        note_pool = [sb.tile([P, U], F32, name=f"note_pool{t}") for t in range(PACK)]
        val_pool = [sb.tile([P, T], F32, name=f"val_pool{t}", tag=f"val_pool{t}", align_bytes=64) for t in range(PACK)]
        before = {t: sb.tile([P, M], F32, name=f"before{t}") for t in (0, 2, 3)}
        put = [sb.tile([P, M], F32, name=f"put{t}") for t in range(PACK)]
        identity = sb.tile([P, P], F32)

        for t in range(PACK):
            nc.vector.memset(put[t][:], 0.0)
        nc.gpsimd.memset(key_bytes[:].bitcast(I32), 0)
        make_identity(nc, identity[:])

        nc.sync.dma_start(tokens[:], offs)
        nc.sync.dma_start(picked_notes[:], offs2)
        nc.sync.dma_start(places[:], offs3)
        nc.sync.dma_start(factors[:], rowf.rearrange("(p t) o -> p (t o)", t=PACK))
        for q in range(4):
            nc.scalar.dma_start(key_bytes[32 * q : 32 * q + 4, :].bitcast(I32), keys_scales[0, 4 * q : 4 * q + 4, :].bitcast(I32))
        for t in range(PACK):
            nc.sync.dma_start(note_pool[t][:], notes_rows[:, t, :])
        nc.sync.dma_start(key_words[:].bitcast(I32), keys_words[0].bitcast(I32))
        for t in range(PACK):
            nc.sync.dma_start(val_pool[t][:], vals_rows[:, t, :])
        for t in (0, 2, 3):
            nc.sync.dma_start(before[t][:], old_rows[:, t, :])

        words_listed = sb.tile([P, I], U16, tag="words_listed", align_bytes=64)
        words_dealt = sb.tile([P, PACK, P], U16, align_bytes=64)
        bytes_dealt = sb.tile([P, PACK, P], U8, align_bytes=64)
        gather_on_vector(nc, bytes_dealt[:].rearrange("p r s -> p s r"), key_bytes[:], tokens[:])

        half = J // 2
        note_planes = sb.tile([P, PACK, J], BF16, tag="note_planes", align_bytes=64)
        for t in range(2):
            gather_on_scalar(nc, note_planes[:, t, :], note_pool[t][:], picked_notes[:])
        gather_on_vector(nc, note_planes[:, 2, :], note_pool[2][:], picked_notes[:])
        last = PACK - 1
        gather_on_vector(nc, note_planes[:, last, :half], note_pool[last][:], picked_notes[:, : LIST_COLS // 2])
        gather_on_scalar(nc, note_planes[:, last, half:], note_pool[last][:], picked_notes[:, LIST_COLS // 2 :])
        gather_on_vector(nc, words_listed[:], key_words[:], tokens[:])
        nc.vector.tensor_copy(words_dealt[:], words_listed[:].rearrange("p (s r) -> p r s", r=PACK))

        note_codes = sb.tile([P, J], U32, tag="words_listed", align_bytes=64)
        note_scales = sb.tile([P, J], U8, align_bytes=64)
        chunks = [slice(c * CHUNK, (c + 1) * CHUNK) for c in range(J // CHUNK)]
        halves = [slice(0, half), slice(half, J)]
        every = slice(0, J)
        notes_woven = [sb.tile([P, CHUNK, PACK], BF16, name=f"notes_woven{c}", align_bytes=64) for c in range(len(chunks))]
        table = [sb.tile([P, half, PACK], BF16, name=f"table{h}", tag=("table0", "relay")[h], align_bytes=64) for h in range(2)]
        table_codes = {}
        table_scales = sb.tile([P, J], U8, align_bytes=64)
        raw = {}

        def score(c):
            nc.vector.quantize_mx(out=note_codes[:, chunks[c]].bitcast(FP8X4), scales=note_scales[:, chunks[c]], in_=notes_woven[c][:].rearrange("p j t -> p (j t)"))
            raw[c] = ps.tile([P, PACK, CHUNK], F32, name="raw", tag="raw", bufs=3)
            for r in range(PACK):
                nc.tensor.matmul_mx(
                    out=raw[c][:, r, :],
                    lhsT=words_dealt[:, r, :].bitcast(FP4X4),
                    lhsT_scale=bytes_dealt[:, r, :],
                    rhs=note_codes[:, chunks[c]].bitcast(FP8X4),
                    rhs_scale=note_scales[:, chunks[c]],
                    start=True,
                    stop=True,
                )

        def weigh(c):
            nc.vector.scalar_tensor_tensor(
                out=table[c // 2][:, chunks[c % 2], :],
                in0=raw[c][:].rearrange("p r j -> p j r"),
                scalar=0.0,
                in1=factors[:].unsqueeze(1).to_broadcast([P, CHUNK, PACK]),
                op0=ALU.max,
                op1=ALU.mult,
            )

        def quantise_table(h, tag):
            table_codes[h] = sb.tile([P, half], U32, name=f"table_codes{h}", tag=tag, align_bytes=64)
            nc.vector.quantize_mx(out=table_codes[h][:].bitcast(FP8X4), scales=table_scales[:, halves[h]], in_=table[h][:].rearrange("p j r -> p (j r)"))

        result = sb.tile([P, PACK, M], F32)
        listed = {}
        woven = {}
        val_codes = {}
        val_scales = {}
        acc = {}
        product = {}

        def gather_values(gather, t, tag):
            listed[t] = sb.tile([P, I], BF16, name=f"listed{t}", tag=tag, align_bytes=64)
            gather(nc, listed[t][:], val_pool[t][:], tokens[:])

        def turn_values(t, bank_tag, into):
            pairs = listed[t][:].bitcast(F32)
            turned = ps.tile([P, 2, P], F32, name="turned", tag=bank_tag, bufs=3 if bank_tag == "raw" else 1)
            for u in range(2):
                nc.tensor.transpose(turned[:, u, :], pairs[:, u : I // 2 : 2], identity[:])
            woven[t] = into.bitcast(BF16)
            nc.vector.tensor_copy(into.rearrange("p (e u) -> p e u", u=2), turned[:].rearrange("p u e -> p e u"))

        def quantise_values(t):
            val_codes[t] = sb.tile([P, P], U32, name=f"val_codes{t}", align_bytes=64)
            val_scales[t] = sb.tile([P, P], U8, name=f"val_scales{t}", align_bytes=64)
            nc.vector.quantize_mx(out=val_codes[t][:].bitcast(FP8X4), scales=val_scales[t][:], in_=woven[t])

        def multiply(t, which, bank_tag):
            bank = ps.tile([P, J], F32, name="acc", tag=bank_tag, bufs=3 if bank_tag == "raw" else 1)
            for h in which:
                nc.tensor.matmul_mx(
                    out=bank[:, halves[h]],
                    lhsT=val_codes[t][:].bitcast(FP8X4),
                    lhsT_scale=val_scales[t][:],
                    rhs=table_codes[h][:].bitcast(FP8X4),
                    rhs_scale=table_scales[:, halves[h]],
                    start=True,
                    stop=True,
                )
                acc[t, h] = bank

        def copy_half(copy, t, h, into):
            copy(into, acc[t, h][:, halves[h]])
            product[t, h] = into

        def copy_whole(copy, t, into):
            copy(into, acc[t, 0][:])
            for h in range(2):
                product[t, h] = into[:, halves[h]]

        def reuse(tag, cols):
            return sb.tile([P, cols], F32, name="reused_" + tag, tag=tag, align_bytes=64)[:]

        def scatter_on_vector(t, h):
            nc.vector.tensor_copy(put[t][:].indirect(places[:, h * 16 : (h + 1) * 16]), product[t, h])

        def scatter_whole_on_vector(t, source):
            nc.vector.tensor_copy(put[t][:].indirect(places[:]), source)

        def scatter_on_scalar(t, h):
            nc.scalar.activation(put[t][:].indirect(places[:, h * 16 : (h + 1) * 16]), product[t, h], COPY)

        def add_and_store(engine, t):
            engine.tensor_tensor(result[:, t, :], before[t][:], put[t][:], ALU.add)
            nc.sync.dma_start(out_rows[:, t, :], result[:, t, :])

        on_vector = nc.vector.tensor_copy
        on_scalar = nc.scalar.copy
        for c in range(len(chunks)):
            weave(on_scalar, notes_woven[c][:], note_planes[:, :, chunks[c]])
        gather_values(gather_on_scalar, 0, "note_planes")
        score(0)
        score(1)
        score(2)
        weigh(0)
        score(3)
        weigh(1)
        turn_values(0, "raw", reuse("woven0", half))
        weigh(2)
        quantise_table(0, "table_codes0")
        quantise_values(0)
        weigh(3)
        gather_values(gather_on_scalar, 1, "listed1")
        multiply(0, [0], "bank_a")
        quantise_table(1, "woven0")
        multiply(0, [1], "bank_b")
        first = reuse("val_pool1", J)
        copy_half(on_scalar, 0, 0, first[:, :half])
        scatter_on_scalar(0, 0)
        copy_half(on_scalar, 0, 1, first[:, half:])
        scatter_on_scalar(0, 1)

        gather_values(gather_on_vector, 2, "relay")
        turn_values(1, "raw", reuse("val_pool2", half))
        quantise_values(1)
        multiply(1, [0, 1], "bank_c")
        gather_values(gather_on_vector, 3, "val_pool2")
        relay = reuse("val_pool3", half + J)
        turn_values(2, "bank_d", relay[:, :half])
        copy_whole(on_vector, 1, relay[:, half:])
        quantise_values(2)
        turn_values(3, "bank_e", reuse("woven3", half))
        before[1] = sb.tile([P, M], F32, name="before1", tag="val_pool2", align_bytes=64)
        nc.sync.dma_start(before[1][:], old_rows[:, 1, :])
        multiply(2, [0, 1], "raw")
        quantise_values(3)
        multiply(3, [0, 1], "raw")
        scatter_on_scalar(1, 0)
        scatter_on_scalar(1, 1)
        third = reuse("woven3", J)
        copy_whole(on_vector, 2, third)
        add_and_store(nc.vector, 0)
        scatter_whole_on_vector(2, third)
        copy_whole(on_scalar, 3, reuse("product3", J))
        scatter_on_scalar(3, 0)
        scatter_on_scalar(3, 1)
        add_and_store(nc.vector, 1)
        add_and_store(nc.vector, 2)
        for c in range(M // OUT_CHUNK):
            cols = slice(c * OUT_CHUNK, (c + 1) * OUT_CHUNK)
            nc.vector.tensor_tensor(result[:, 3, cols], before[3][:, cols], put[3][:, cols], ALU.add)
            if c % 2 == 1:
                both = slice((c - 1) * OUT_CHUNK, (c + 1) * OUT_CHUNK)
                nc.sync.dma_start(out_rows[:, 3, both], result[:, 3, both])

        result_codes = sb.tile([P, M], U32, align_bytes=64)
        result_scales = sb.tile([P, M], U8, align_bytes=64)
        for c in range(M // OUT_CHUNK):
            cols = slice(c * OUT_CHUNK, (c + 1) * OUT_CHUNK)
            rounded = sb.tile([P, OUT_CHUNK, PACK], BF16, name=f"rounded{c}", align_bytes=64)
            weave(nc.scalar.copy if c % 2 == 0 else nc.vector.tensor_copy, rounded[:], result[:, :, cols])
            nc.vector.quantize_mx(out=result_codes[:, cols].bitcast(FP8X4), scales=result_scales[:, cols], in_=rounded[:].rearrange("p m t -> p (m t)"))
            nc.sync.dma_start(out_words[:, cols], result_codes[:, cols].bitcast(I32))
        for q in range(4):
            queue = nc.sync if q % 2 == 0 else nc.scalar
            queue.dma_start(out_2[0, 4 * q : 4 * q + 4, :].bitcast(I32), result_scales[32 * q : 32 * q + 4, :].bitcast(I32))
